import numpy as np
import ml_dtypes

BF16 = ml_dtypes.bfloat16


def bf(x):
    return np.asarray(x, np.float32).astype(BF16)


def f32(x):
    return np.asarray(x, np.float32)


def f64(x):
    return np.asarray(x).astype(np.float64)


def striped(idx):
    return np.tile(idx.reshape(-1, 16).T, (8, 1))


S, K, M, N = 512, 128, 128, 256


def setup_inputs():
    return {"base": bf(np.random.standard_normal((M, S))), "x": bf(np.random.standard_normal((K, N))), "w": bf(np.random.standard_normal((K, M)) / np.sqrt(K)), "b": f32(0.5 * np.random.standard_normal((M, 1))), "offs": striped(np.random.permutation(S)[:N])}


def reference(base, x, w, b, offs):
    idx = offs[:16].T.reshape(-1)
    z = f64(base).copy()
    z[:, idx] += f64(w).T @ f64(x)
    return np.tanh(z + f64(b))

@@ -1,0 +1,37 @@
+import concourse.mybir as mybir
+from concourse.masks import make_identity
+
+BF16, F32, U16 = mybir.dt.bfloat16, mybir.dt.float32, mybir.dt.uint16
+TANH = mybir.ActivationFunctionType.Tanh
+
+K, M, N, S = 128, 128, 256, 512
+FLOPS = 2 * K * M * N
+
+
+def tile_scatter_matmul_kernel(tc, base, x, w, b, offs, out):
+    nc = tc.nc
+    with (
+        tc.tile_pool(name="held", bufs=1) as held,
+        tc.psum_pool(name="psum", bufs=1) as psum,
+    ):
+        base_tile = held.tile([M, S], BF16)
+        weights = held.tile([K, M], BF16)
+        moving = held.tile([K, N], BF16)
+        offsets = held.tile([128, N // 16], U16)
+        bias = held.tile([M, 1], F32)
+        identity = held.tile([M, M], BF16)
+        result = held.tile([M, S], F32)
+        window = psum.tile([M, S], F32)
+
+        nc.sync.dma_start(base_tile[:], base)
+        nc.sync.dma_start(moving[:], x)
+        nc.sync.dma_start(weights[:], w)
+        nc.sync.dma_start(offsets[:], offs)
+        nc.sync.dma_start(bias[:], b)
+        make_identity(nc, identity[:])
+
+        nc.tensor.matmul(window[:], identity[:], base_tile[:], start=True, stop=False)
+        nc.tensor.matmul(window[:].indirect(offsets[:]), weights[:], moving[:], start=False, stop=True)
+
+        nc.scalar.activation(result[:], window[:], TANH, bias=bias[:])
+        nc.sync.dma_start(out, result[:])

@@ -21,6 +21,7 @@ def tile_scatter_matmul_kernel(tc, base, x, w, b, offs, out):
         bias = held.tile([M, 1], F32)
         identity = held.tile([M, M], BF16)
         result = held.tile([M, S], F32)
+        scratch = held.tile([M, 1], F32)
         window = psum.tile([M, S], F32)
 
         nc.sync.dma_start(base_tile[:], base)
@@ -29,6 +30,9 @@ def tile_scatter_matmul_kernel(tc, base, x, w, b, offs, out):
         nc.sync.dma_start(offsets[:], offs)
         nc.sync.dma_start(bias[:], b)
         make_identity(nc, identity[:])
+
+        nc.vector.memset(scratch[:], 0.0)
+        nc.scalar.activation(scratch[:], scratch[:], TANH)
 
         nc.tensor.matmul(window[:], identity[:], base_tile[:], start=True, stop=False)
         nc.tensor.matmul(window[:].indirect(offsets[:]), weights[:], moving[:], start=False, stop=True)

import concourse.mybir as mybir
from concourse.masks import make_identity

BF16, F32, U16 = mybir.dt.bfloat16, mybir.dt.float32, mybir.dt.uint16
TANH = mybir.ActivationFunctionType.Tanh

K, M, N, S = 128, 128, 256, 512
FLOPS = 2 * K * M * N


def tile_scatter_matmul_kernel(tc, base, x, w, b, offs, out):
    nc = tc.nc
    with (
        tc.tile_pool(name="held", bufs=1) as held,
        tc.psum_pool(name="psum", bufs=1) as psum,
    ):
        base_tile = held.tile([M, S], BF16)
        weights = held.tile([K, M], BF16)
        moving = held.tile([K, N], BF16)
        offsets = held.tile([128, N // 16], U16)
        bias = held.tile([M, 1], F32)
        identity = held.tile([M, M], BF16)
        result = held.tile([M, S], F32)
        scratch = held.tile([M, 1], F32)
        window = psum.tile([M, S], F32)

        nc.sync.dma_start(base_tile[:], base)
        nc.sync.dma_start(moving[:], x)
        nc.sync.dma_start(weights[:], w)
        nc.sync.dma_start(offsets[:], offs)
        nc.sync.dma_start(bias[:], b)
        make_identity(nc, identity[:])

        nc.vector.memset(scratch[:], 0.0)
        nc.scalar.activation(scratch[:], scratch[:], TANH)

        nc.tensor.matmul(window[:], identity[:], base_tile[:], start=True, stop=False)
        nc.tensor.matmul(window[:].indirect(offsets[:]), weights[:], moving[:], start=False, stop=True)

        nc.scalar.activation(result[:], window[:], TANH, bias=bias[:])
        nc.sync.dma_start(out, result[:])
